import numpy as np
import ml_dtypes


def mxq(x, axis, fmt="e4m3"):
    dtype, down = {"e4m3": (ml_dtypes.float8_e4m3fn, 7), "e5m2": (ml_dtypes.float8_e5m2, 14)}[fmt]
    v = np.moveaxis(np.asarray(x, np.float32).astype(ml_dtypes.bfloat16).astype(np.float64), axis, -1)
    blocks = v.reshape(v.shape[:-1] + (-1, 32))
    amax = np.abs(blocks).max(-1, keepdims=True)
    byte = np.maximum(np.where(amax > 0, np.frexp(amax)[1] - 1 + 127, 0) - down, 1)
    scale = np.exp2(byte - 127.0)
    codes = (blocks / scale).astype(np.float32).astype(dtype).astype(np.float64)
    return np.moveaxis((codes * scale).reshape(v.shape), -1, axis)


WIDE = False


def mx_kscale(k):
    if not WIDE:
        return np.ones(k)
    levels = np.array([10, -10, 5, -5, 0])
    if k % 512:
        return np.exp2(np.random.permutation(np.resize(levels, k // 32))).repeat(32)
    a = np.empty((k // 512, 16))
    for p in range(k // 512):
        a[p, :8] = np.random.permutation(np.resize(levels, 8))
        for g in range(8):
            far = levels[np.abs(levels - a[p, g]) >= 10]
            a[p, g + 8] = far[np.random.randint(len(far))]
    return np.exp2(a.ravel()).repeat(32)


def f64(x):
    return np.asarray(x).astype(np.float64)


def striped(idx):
    return np.tile(idx.reshape(-1, 16).T, (8, 1)).astype(np.uint16)


def unstriped(offs):
    return offs[:16].T.reshape(-1).astype(np.int64)


E2M1 = np.array([0.0, 0.5, 1.0, 1.5, 2.0, 3.0, 4.0, 6.0, -0.0, -0.5, -1.0, -1.5, -2.0, -3.0, -4.0, -6.0])


def pack_weight(w, fmt):
    k, n = w.shape
    w = f64(np.asarray(w, np.float32).astype(ml_dtypes.bfloat16)).reshape(k // 32, 32, n)
    amax = np.abs(w).max(1)
    if fmt == "e4m3":
        byte = np.frexp(amax)[1] - 1 + 127 - 7
    else:
        mant, ex = np.frexp(amax / 6.0)
        byte = np.where(mant > 0.5, ex, ex - 1) + 127
    byte = np.clip(np.where(amax > 0, byte, 1), 1, 254)
    scaled = (w * np.exp2(127.0 - byte)[:, None, :]).reshape(k, n).astype(np.float32)
    by_word = np.ascontiguousarray(scaled.reshape(k // 512, 128, 4, n).transpose(0, 1, 3, 2))
    if fmt == "e4m3":
        words = by_word.astype(ml_dtypes.float8_e4m3fn).view(np.uint8)
    else:
        c = by_word.astype(ml_dtypes.float4_e2m1fn).view(np.uint8) & 0xF
        words = (c[..., 0::2] | (c[..., 1::2] << 4)).reshape(k // 512, 128, 2 * n)
    return np.ascontiguousarray(words), np.ascontiguousarray(byte.astype(np.uint8).reshape(k // 512, 16, n))


def unpack_weight(words, scales, fmt):
    g, _, n = scales.shape
    words = np.ascontiguousarray(words).reshape(g, 128, n, -1)
    if fmt == "e4m3":
        vals = words.view(ml_dtypes.float8_e4m3fn).astype(np.float64)
    else:
        nib = np.empty((g, 128, n, 4), np.uint8)
        nib[..., 0::2] = words & 0xF
        nib[..., 1::2] = words >> 4
        vals = E2M1[nib]
    vals = vals * np.repeat(np.exp2(scales.astype(np.float64) - 127.0), 8, axis=1)[..., None]
    return vals.transpose(0, 1, 3, 2).reshape(g * 512, n)


def gelu(v):
    return 0.5 * v * (1.0 + np.tanh(np.sqrt(2.0 / np.pi) * (v + 0.044715 * v**3)))


K, H, N, T, S, P1, P2, P3 = 1024, 512, 768, 4096, 2048, 1024, 512, 256


def setup_inputs():
    n = np.random.standard_normal
    s = mx_kscale(K)[:, None]
    u = mx_kscale(H)[:, None]
    tab_words, tab_scales = pack_weight(n((K, T)) * s, "e4m3")
    w2_words, w2_scales = pack_weight(0.55 * n((K, H)) / np.sqrt(K) / s, "e2m1")
    return {
        "tab_words": tab_words, "tab_scales": tab_scales,
        "offs": striped(np.random.permutation(T)[:S]),
        "w1": (0.8 * n((K, H)) / np.sqrt(K) / s * u.T).astype(np.float32),
        "w2_words": w2_words, "w2_scales": w2_scales,
        "d": (2.2 * np.exp(0.3 * n(H)) * u[:, 0]).astype(np.float32),
        "pos1": striped(np.random.permutation(S)[:P1]),
        "pos2": striped(np.random.permutation(S)[:P1]),
        "pos3": striped(np.random.permutation(P1)[:P2]),
        "pos4": striped(np.random.permutation(P1)[:P2]),
        "pos5": striped(np.random.permutation(P2)[:P3]),
        "pos6": striped(np.random.permutation(P2)[:P3]),
        "w3": (1.5 * n((H, N)) / np.sqrt(H) / u**2).astype(np.float32),
    }


def reference(tab_words, tab_scales, offs, w1, w2_words, w2_scales, d,
              pos1, pos2, pos3, pos4, pos5, pos6, w3):
    v = unpack_weight(tab_words, tab_scales, "e4m3")[:, unstriped(offs)]
    w2 = unpack_weight(w2_words, w2_scales, "e2m1")
    b1 = mxq(f64(w1), 0, "e4m3").T @ v
    b2 = w2.T @ v
    h = np.maximum(b1, f64(d)[:, None] * np.sin(b2))
    a1 = h[:, unstriped(pos1)] + h[:, unstriped(pos2)]
    a2 = a1[:, unstriped(pos3)] * a1[:, unstriped(pos4)]
    a3 = np.minimum(a2[:, unstriped(pos5)], a2[:, unstriped(pos6)])
    y = mxq(f64(w3), 0, "e4m3").T @ mxq(a3, 0, "e4m3")
    return 1.0 / (1.0 + np.exp(-y))

@@ -1,0 +1,283 @@
+from contextlib import ExitStack
+
+import concourse.mybir as mybir
+
+K, H, N, T, S, P1, P2, P3 = 1024, 512, 768, 4096, 2048, 1024, 512, 256
+FLOPS = 2 * (2 * K * H * S + H * N * P3)
+
+F32 = mybir.dt.float32
+BF16 = mybir.dt.bfloat16
+I32 = mybir.dt.int32
+U32 = mybir.dt.uint32
+U16 = mybir.dt.uint16
+U8 = mybir.dt.uint8
+FP8X4 = mybir.dt.float8_e4m3fn_x4
+FP4X4 = mybir.dt.float4_e2m1fn_x4
+ALU = mybir.AluOpType
+ACT = mybir.ActivationFunctionType
+
+P = 128
+PACK = 4
+PASSES = K // (P * PACK)
+CHUNK = 512
+CHUNKS = S // CHUNK
+PER_COLUMN = 16
+SCALE_ROWS = 16
+QUADRANT = 32
+HALF = P3 // 2
+OUT_TILES = N // P
+TILES_PER_BANK = 3
+
+
+def tile_list_qualifier_seed_features_kernel(
+    tc, tab_words, tab_scales, offs, w1, w2_words, w2_scales, d, pos1, pos2, pos3, pos4, pos5, pos6, w3, out
+):
+    nc = tc.nc
+    with ExitStack() as ctx:
+        lists = ctx.enter_context(tc.tile_pool(name="lists", bufs=1))
+        keep = ctx.enter_context(tc.tile_pool(name="keep", bufs=1))
+        work = ctx.enter_context(tc.tile_pool(name="work", bufs=2))
+        psum = ctx.enter_context(tc.psum_pool(name="psum", bufs=1))
+
+        def load_list(name, source):
+            tile = lists.tile(list(source.shape), U16, name=name)
+            nc.sync.dma_start(tile[:], source)
+            return tile
+
+        idx = load_list("idx", offs)
+
+        scale_table = keep.tile([P, T // 4], I32, name="scale_table", tag="early", align_bytes=64)
+        nc.sync.dma_start(
+            scale_table[0 : PASSES * SCALE_ROWS, :], tab_scales.rearrange("a q t -> (a q) t").bitcast(I32)
+        )
+        nc.vector.memset(scale_table[32:64, :], 0)
+        nc.vector.memset(scale_table[64:128, :], 0)
+
+        w2_scales_raw = keep.tile([P, PASSES, H], U8, name="w2_scales_raw", align_bytes=64)
+        nc.vector.memset(w2_scales_raw[:].bitcast(I32), 0)
+        v_scales = keep.tile([P, PASSES, S], U8, name="v_scales", align_bytes=64)
+        nc.vector.memset(v_scales[:].bitcast(I32), 0)
+
+        word_tables = []
+        for a in range(PASSES):
+            table = keep.tile([P, T], I32, name=f"word_table{a}", tag=f"table{a}", align_bytes=64)
+            nc.sync.dma_start(table[:], tab_words[a].rearrange("p t i -> p (t i)").bitcast(I32))
+            word_tables.append(table)
+            if a == 0:
+                w2_raw = keep.tile([P, PASSES, H // 2], I32, name="w2_raw", align_bytes=64)
+                nc.sync.dma_start(w2_raw[:], w2_words.rearrange("a p c -> p a c").bitcast(I32))
+
+        for r in range(4):
+            nc.scalar.dma_start(
+                w2_scales_raw[r:P:QUADRANT, :, :].bitcast(I32),
+                w2_scales.rearrange("a (q r) c -> r q a c", r=4)[r].bitcast(I32),
+            )
+        d_cols = keep.tile([P, PACK], F32, name="d_cols")
+        nc.scalar.dma_start(d_cols[:], d.rearrange("(p t) -> p t", t=PACK))
+
+        picked_scales = keep.tile([P, S], U8, name="picked_scales", align_bytes=64)
+        nc.vector.tensor_copy(picked_scales[:], scale_table[:].bitcast(U8).indirect(idx[:]))
+        for a in range(PASSES):
+            for q in range(4):
+                row = SCALE_ROWS * a + 4 * q
+                nc.scalar.dma_start(
+                    v_scales[QUADRANT * q : QUADRANT * q + 4, a, :].bitcast(I32),
+                    picked_scales[row : row + 4, :].bitcast(I32),
+                )
+
+        w1_raw = keep.tile([P, PASSES, PACK, H], F32, name="w1_raw", tag="early", align_bytes=64)
+        for a in range(PASSES):
+            nc.sync.dma_start(
+                w1_raw[:, a], w1[a * P * PACK : (a + 1) * P * PACK, :].rearrange("(p j) c -> p j c", j=PACK)
+            )
+
+        p1, p2, p3, p4, p5, p6 = [
+            load_list(f"pair_list{i}", source) for i, source in enumerate((pos1, pos2, pos3, pos4, pos5, pos6))
+        ]
+
+        v_words = [[None] * CHUNKS for a in range(PASSES)]
+
+        def pick_words(a, c):
+            picked = keep.tile([P, CHUNK], U32, name=f"v_words{a}_{c}", align_bytes=64)
+            columns = CHUNK // PER_COLUMN
+            nc.vector.tensor_copy(
+                picked[:], word_tables[a][:].bitcast(U32).indirect(idx[:, c * columns : (c + 1) * columns])
+            )
+            v_words[a][c] = picked
+
+        for c in range(CHUNKS):
+            pick_words(0, c)
+
+        w2_codes = keep.tile([P, PASSES, PACK, P], U16, name="w2_codes", align_bytes=64)
+        nc.vector.tensor_copy(w2_codes[:], w2_raw[:].bitcast(U16).rearrange("p a (m t) -> p a t m", t=PACK))
+        w2_plane = keep.tile([P, PASSES, PACK, P], U8, name="w2_plane", align_bytes=64)
+        nc.vector.tensor_copy(w2_plane[:], w2_scales_raw[:].rearrange("p a (m t) -> p a t m", t=PACK))
+
+        for c in range(CHUNKS):
+            pick_words(1, c)
+
+        w1_codes = keep.tile([P, PASSES, PACK, P], U32, name="w1_codes", align_bytes=64)
+        w1_plane = keep.tile([P, PASSES, PACK, P], U8, name="w1_plane", align_bytes=64)
+
+        def quantise_w1(a, t0, t1):
+            tiles = t1 - t0
+            rounded = keep.tile([P, tiles, P, PACK], BF16, name=f"w1_rounded{a}_{t0}", align_bytes=64)
+            nc.scalar.copy(
+                rounded[:].rearrange("p t m j -> p m j t"),
+                w1_raw[:, a].rearrange("p j (m t) -> p m j t", t=PACK)[:, :, :, t0:t1],
+            )
+            nc.vector.quantize_mx(
+                out=w1_codes[:, a, t0:t1, :].rearrange("p t m -> p (t m)").bitcast(FP8X4),
+                scales=w1_plane[:, a, t0:t1, :].rearrange("p t m -> p (t m)"),
+                in_=rounded[:].rearrange("p t m j -> p (t m j)"),
+            )
+
+        quantise_w1(0, 0, PACK)
+        quantise_w1(1, 0, 1)
+
+        w3_raw = keep.tile([P, PACK, N], F32, name="w3_raw", tag="table0", align_bytes=64)
+        nc.sync.dma_start(w3_raw[:], w3.rearrange("(p t) n -> p t n", t=PACK))
+        w3_codes = keep.tile([P, N], U32, name="w3_codes", align_bytes=64)
+        w3_plane = keep.tile([P, N], U8, name="w3_plane", align_bytes=64)
+
+        def quantise_w3(b):
+            width = TILES_PER_BANK * P
+            cols = slice(b * width, (b + 1) * width)
+            rounded = keep.tile([P, width, PACK], BF16, name=f"w3_rounded{b}", align_bytes=64)
+            nc.scalar.copy(rounded[:], w3_raw[:, :, cols].rearrange("p t n -> p n t"))
+            nc.vector.quantize_mx(
+                out=w3_codes[:, cols].bitcast(FP8X4),
+                scales=w3_plane[:, cols],
+                in_=rounded[:].rearrange("p n t -> p (n t)"),
+            )
+
+        h = [keep.tile([P, S], F32, name=f"h{t}") for t in range(PACK)]
+        a1 = [keep.tile([P, P1], F32, name=f"a1_{t}") for t in range(PACK)]
+        a2 = [keep.tile([P, P2], F32, name=f"a2_{t}") for t in range(PACK)]
+        a3 = keep.tile([P, PACK, P3], BF16, name="a3", align_bytes=64)
+        first = {}
+
+        def reading(t, c):
+            cols = slice(c * CHUNK, (c + 1) * CHUNK)
+            b2 = psum.tile([P, CHUNK], F32, name="b2", tag="short", bufs=2)
+            for a in range(PASSES):
+                nc.tensor.matmul_mx(
+                    out=b2[:],
+                    lhsT=w2_codes[:, a, t, :].bitcast(U8).bitcast(FP4X4),
+                    lhsT_scale=w2_plane[:, a, t, :],
+                    rhs=v_words[a][c][:].bitcast(FP8X4),
+                    rhs_scale=v_scales[:, a, cols],
+                    start=(a == 0),
+                    stop=(a == PASSES - 1),
+                )
+            sine = work.tile([P, CHUNK], F32, name="sine", bufs=6)
+            nc.scalar.activation(sine[:], b2[:], ACT.Sin)
+            b1 = psum.tile([P, CHUNK], F32, name="b1", tag="long", bufs=6)
+            for a in range(PASSES):
+                nc.tensor.matmul_mx(
+                    out=b1[:],
+                    lhsT=w1_codes[:, a, t, :].bitcast(FP8X4),
+                    lhsT_scale=w1_plane[:, a, t, :],
+                    rhs=v_words[a][c][:].bitcast(FP8X4),
+                    rhs_scale=v_scales[:, a, cols],
+                    start=(a == 0),
+                    stop=(a == PASSES - 1),
+                )
+            nc.vector.scalar_tensor_tensor(
+                out=h[t][:, cols], in0=sine[:], scalar=d_cols[:, t : t + 1], in1=b1[:], op0=ALU.mult, op1=ALU.max
+            )
+
+        def pick(key, window, offsets):
+            width = offsets.shape[1] * PER_COLUMN
+            picked = work.tile([P, width], F32, name=f"picked_{key[0]}_{width}")
+            nc.vector.tensor_copy(picked[:], window[:].indirect(offsets))
+            first[key] = picked
+
+        def pick_and_combine(result, key, window, offsets, op):
+            nc.vector.tensor_tensor(result[:], window[:].indirect(offsets), first[key][:], op)
+
+        def smaller(t, j0, j1):
+            nc.vector.tensor_tensor(a3[:, t, j0:j1], first["e", t, j0][:], first["f", t, j0][:], ALU.min)
+
+        def list_part(tile, j0, j1):
+            return tile[:, j0 // PER_COLUMN : j1 // PER_COLUMN]
+
+        def interleave(half):
+            grouped = keep.tile([P, HALF, PACK], BF16, name=f"a3_grouped{half}", align_bytes=64)
+            nc.vector.tensor_copy(grouped[:], a3[:, :, half * HALF : (half + 1) * HALF].rearrange("p t j -> p j t"))
+            first["g", half] = grouped
+
+        def features(half):
+            codes = keep.tile([P, HALF], U32, name=f"a3_codes{half}", align_bytes=64)
+            plane = keep.tile([P, HALF], U8, name=f"a3_plane{half}", align_bytes=64)
+            nc.vector.quantize_mx(
+                out=codes[:].bitcast(FP8X4), scales=plane[:], in_=first["g", half][:].rearrange("p j t -> p (j t)")
+            )
+            for b in range(OUT_TILES // TILES_PER_BANK):
+                y = psum.tile([P, CHUNK], F32, name="y", tag="short", bufs=2)
+                for u in range(TILES_PER_BANK):
+                    rows = slice((b * TILES_PER_BANK + u) * P, (b * TILES_PER_BANK + u + 1) * P)
+                    nc.tensor.matmul_mx(
+                        out=y[:, u * HALF : (u + 1) * HALF],
+                        lhsT=w3_codes[:, rows].bitcast(FP8X4),
+                        lhsT_scale=w3_plane[:, rows],
+                        rhs=codes[:].bitcast(FP8X4),
+                        rhs_scale=plane[:],
+                        start=True,
+                        stop=True,
+                    )
+                result = work.tile([P, TILES_PER_BANK * HALF], F32, name="result", bufs=4)
+                nc.scalar.activation(result[:], y[:, 0 : TILES_PER_BANK * HALF], ACT.Sigmoid)
+                nc.sync.dma_start(
+                    out.rearrange("(u p) j -> p u j", p=P)[
+                        :, b * TILES_PER_BANK : (b + 1) * TILES_PER_BANK, half * HALF : (half + 1) * HALF
+                    ],
+                    result[:].rearrange("p (u j) -> p u j", j=HALF),
+                )
+
+        reading(0, 0)
+        quantise_w1(1, 1, PACK)
+        for c in range(1, CHUNKS):
+            reading(0, c)
+        reading(1, 0)
+
+        last = PACK - 1
+        for t in range(PACK):
+            pick(("a", t), h[t], p1[:])
+            if t == 0:
+                reading(1, 1)
+            else:
+                pick(("c", t - 1), a1[t - 1], p3[:])
+            pick_and_combine(a1[t], ("a", t), h[t], p2[:], ALU.add)
+            if t == 0:
+                reading(1, 2)
+                reading(1, 3)
+                quantise_w3(0)
+                continue
+            pick_and_combine(a2[t - 1], ("c", t - 1), a1[t - 1], p4[:], ALU.mult)
+            if t < last:
+                reading(t + 1, 0)
+            else:
+                pick(("c", t), a1[t], p3[:])
+            pick(("e", t - 1, 0), a2[t - 1], p5[:])
+            if t == last:
+                pick_and_combine(a2[t], ("c", t), a1[t], p4[:], ALU.mult)
+            pick(("f", t - 1, 0), a2[t - 1], p6[:])
+            if t < last:
+                for c in range(1, CHUNKS):
+                    reading(t + 1, c)
+            else:
+                pick(("e", t, 0), a2[t], list_part(p5, 0, HALF))
+            smaller(t - 1, 0, P3)
+            if t == 1:
+                quantise_w3(1)
+
+        pick(("f", last, 0), a2[last], list_part(p6, 0, HALF))
+        pick(("e", last, HALF), a2[last], list_part(p5, HALF, P3))
+        smaller(last, 0, HALF)
+        pick(("f", last, HALF), a2[last], list_part(p6, HALF, P3))
+        interleave(0)
+        smaller(last, HALF, P3)
+        features(0)
+        interleave(1)
+        features(1)

@@ -26,7 +26,9 @@ SCALE_ROWS = 16
 QUADRANT = 32
 HALF = P3 // 2
 OUT_TILES = N // P
-TILES_PER_BANK = 3
+TILES_PER_BANK = 2
+FIRST_ROW = P - PASSES * SCALE_ROWS
+W3_PARTS = 2
 
 
 def tile_list_qualifier_seed_features_kernel(
@@ -45,95 +47,95 @@ def tile_list_qualifier_seed_features_kernel(
             return tile
 
         idx = load_list("idx", offs)
-
-        scale_table = keep.tile([P, T // 4], I32, name="scale_table", tag="early", align_bytes=64)
-        nc.sync.dma_start(
-            scale_table[0 : PASSES * SCALE_ROWS, :], tab_scales.rearrange("a q t -> (a q) t").bitcast(I32)
-        )
-        nc.vector.memset(scale_table[32:64, :], 0)
-        nc.vector.memset(scale_table[64:128, :], 0)
-
+        scale_table = keep.tile([P, T // 4], I32, name="scale_table", align_bytes=64)
+        nc.sync.dma_start(scale_table[FIRST_ROW:P, :], tab_scales.rearrange("a q t -> (a q) t").bitcast(I32))
         w2_scales_raw = keep.tile([P, PASSES, H], U8, name="w2_scales_raw", align_bytes=64)
         nc.vector.memset(w2_scales_raw[:].bitcast(I32), 0)
+        nc.vector.memset(scale_table[0:FIRST_ROW, :], 0)
         v_scales = keep.tile([P, PASSES, S], U8, name="v_scales", align_bytes=64)
         nc.vector.memset(v_scales[:].bitcast(I32), 0)
 
-        word_tables = []
+        word_tables = [
+            keep.tile([P, T], I32, name=f"word_table{a}", tag=f"table{a}", align_bytes=64) for a in range(PASSES)
+        ]
+        word_rows = [tab_words[a].rearrange("p t i -> p (t i)").bitcast(I32) for a in range(PASSES)]
         for a in range(PASSES):
-            table = keep.tile([P, T], I32, name=f"word_table{a}", tag=f"table{a}", align_bytes=64)
-            nc.sync.dma_start(table[:], tab_words[a].rearrange("p t i -> p (t i)").bitcast(I32))
-            word_tables.append(table)
-            if a == 0:
-                w2_raw = keep.tile([P, PASSES, H // 2], I32, name="w2_raw", align_bytes=64)
-                nc.sync.dma_start(w2_raw[:], w2_words.rearrange("a p c -> p a c").bitcast(I32))
+            nc.sync.dma_start(word_tables[a][:, 0 : T // 2], word_rows[a][:, 0 : T // 2])
 
+        w2_raw = keep.tile([P, PASSES, H // 2], I32, name="w2_raw", align_bytes=64)
+        nc.scalar.dma_start(w2_raw[:], w2_words.rearrange("a p c -> p a c").bitcast(I32))
+        d_cols = keep.tile([P, PACK], F32, name="d_cols")
+        nc.scalar.dma_start(d_cols[:], d.rearrange("(p t) -> p t", t=PACK))
         for r in range(4):
             nc.scalar.dma_start(
                 w2_scales_raw[r:P:QUADRANT, :, :].bitcast(I32),
                 w2_scales.rearrange("a (q r) c -> r q a c", r=4)[r].bitcast(I32),
             )
-        d_cols = keep.tile([P, PACK], F32, name="d_cols")
-        nc.scalar.dma_start(d_cols[:], d.rearrange("(p t) -> p t", t=PACK))
+        for a in range(PASSES):
+            nc.scalar.dma_start(word_tables[a][:, T // 2 : T], word_rows[a][:, T // 2 : T])
 
         picked_scales = keep.tile([P, S], U8, name="picked_scales", align_bytes=64)
         nc.vector.tensor_copy(picked_scales[:], scale_table[:].bitcast(U8).indirect(idx[:]))
         for a in range(PASSES):
             for q in range(4):
-                row = SCALE_ROWS * a + 4 * q
-                nc.scalar.dma_start(
+                row = FIRST_ROW + SCALE_ROWS * a + 4 * q
+                queue = nc.sync if 4 * a + q < 2 else nc.scalar
+                queue.dma_start(
                     v_scales[QUADRANT * q : QUADRANT * q + 4, a, :].bitcast(I32),
                     picked_scales[row : row + 4, :].bitcast(I32),
                 )
 
-        w1_raw = keep.tile([P, PASSES, PACK, H], F32, name="w1_raw", tag="early", align_bytes=64)
+        w1_raw = keep.tile([P, PASSES, PACK, H], F32, name="w1_raw", align_bytes=64)
         for a in range(PASSES):
             nc.sync.dma_start(
                 w1_raw[:, a], w1[a * P * PACK : (a + 1) * P * PACK, :].rearrange("(p j) c -> p j c", j=PACK)
             )
-
         p1, p2, p3, p4, p5, p6 = [
-            load_list(f"pair_list{i}", source) for i, source in enumerate((pos1, pos2, pos3, pos4, pos5, pos6))
+            load_list(f"p{i + 1}", source) for i, source in enumerate((pos1, pos2, pos3, pos4, pos5, pos6))
         ]
 
         v_words = [[None] * CHUNKS for a in range(PASSES)]
 
         def pick_words(a, c):
-            picked = keep.tile([P, CHUNK], U32, name=f"v_words{a}_{c}", align_bytes=64)
+            picked = keep.tile([P, CHUNK], U32, name=f"v_words{a}_{c}", tag=f"v_words{a}_{c}", align_bytes=64)
             columns = CHUNK // PER_COLUMN
             nc.vector.tensor_copy(
                 picked[:], word_tables[a][:].bitcast(U32).indirect(idx[:, c * columns : (c + 1) * columns])
             )
             v_words[a][c] = picked
 
+        w2_plane = keep.tile([P, PASSES, PACK, P], U8, name="w2_plane", align_bytes=64)
+        nc.vector.tensor_copy(w2_plane[:], w2_scales_raw[:].rearrange("p a (m t) -> p a t m", t=PACK))
+        w2_codes = keep.tile([P, PASSES, PACK, P], U16, name="w2_codes", align_bytes=64)
+        nc.vector.tensor_copy(w2_codes[:], w2_raw[:].bitcast(U16).rearrange("p a (m t) -> p a t m", t=PACK))
         for c in range(CHUNKS):
             pick_words(0, c)
 
-        w2_codes = keep.tile([P, PASSES, PACK, P], U16, name="w2_codes", align_bytes=64)
-        nc.vector.tensor_copy(w2_codes[:], w2_raw[:].bitcast(U16).rearrange("p a (m t) -> p a t m", t=PACK))
-        w2_plane = keep.tile([P, PASSES, PACK, P], U8, name="w2_plane", align_bytes=64)
-        nc.vector.tensor_copy(w2_plane[:], w2_scales_raw[:].rearrange("p a (m t) -> p a t m", t=PACK))
+        w1_codes = keep.tile([P, PACK, PASSES, P], U32, name="w1_codes", align_bytes=64)
+        w1_plane = keep.tile([P, PACK, PASSES, P], U8, name="w1_plane", align_bytes=64)
 
-        for c in range(CHUNKS):
-            pick_words(1, c)
+        sines = {}
 
-        w1_codes = keep.tile([P, PASSES, PACK, P], U32, name="w1_codes", align_bytes=64)
-        w1_plane = keep.tile([P, PASSES, PACK, P], U8, name="w1_plane", align_bytes=64)
-
-        def quantise_w1(a, t0, t1):
-            tiles = t1 - t0
-            rounded = keep.tile([P, tiles, P, PACK], BF16, name=f"w1_rounded{a}_{t0}", align_bytes=64)
-            nc.scalar.copy(
-                rounded[:].rearrange("p t m j -> p m j t"),
-                w1_raw[:, a].rearrange("p j (m t) -> p m j t", t=PACK)[:, :, :, t0:t1],
-            )
+        def quantise_w1(t, a0, a1, tag):
+            rounded = keep.tile([P, a1 - a0, P, PACK], BF16, name=f"w1_rounded{t}_{a0}", tag=tag, align_bytes=64)
+            for a in range(a0, a1):
+                nc.scalar.copy(rounded[:, a - a0], w1_raw[:, a].rearrange("p j (m t) -> p t m j", t=PACK)[:, t])
             nc.vector.quantize_mx(
-                out=w1_codes[:, a, t0:t1, :].rearrange("p t m -> p (t m)").bitcast(FP8X4),
-                scales=w1_plane[:, a, t0:t1, :].rearrange("p t m -> p (t m)"),
-                in_=rounded[:].rearrange("p t m j -> p (t m j)"),
+                out=w1_codes[:, t, a0:a1].rearrange("p a m -> p (a m)").bitcast(FP8X4),
+                scales=w1_plane[:, t, a0:a1].rearrange("p a m -> p (a m)"),
+                in_=rounded[:].rearrange("p a m j -> p (a m j)"),
             )
 
-        quantise_w1(0, 0, PACK)
-        quantise_w1(1, 0, 1)
+        def prepare(t, a0):
+            quantise_w1(t, a0, PASSES, f"turn{t % 2}")
+            sines[t] = keep.tile([P, S], F32, name=f"sines{t}", tag=f"turn{t % 2}", align_bytes=64)
+
+        pick_words(1, 0)
+        pick_words(1, 1)
+        quantise_w1(0, 0, 1, "v_words1_2")
+        pick_words(1, 2)
+        pick_words(1, 3)
+        prepare(0, 1)
 
         w3_raw = keep.tile([P, PACK, N], F32, name="w3_raw", tag="table0", align_bytes=64)
         nc.sync.dma_start(w3_raw[:], w3.rearrange("(p t) n -> p t n", t=PACK))
@@ -141,9 +143,9 @@ def tile_list_qualifier_seed_features_kernel(
         w3_plane = keep.tile([P, N], U8, name="w3_plane", align_bytes=64)
 
         def quantise_w3(b):
-            width = TILES_PER_BANK * P
+            width = N // W3_PARTS
             cols = slice(b * width, (b + 1) * width)
-            rounded = keep.tile([P, width, PACK], BF16, name=f"w3_rounded{b}", align_bytes=64)
+            rounded = keep.tile([P, width, PACK], BF16, name=f"w3_rounded{b}", tag=f"v_words0_{b}", align_bytes=64)
             nc.scalar.copy(rounded[:], w3_raw[:, :, cols].rearrange("p t n -> p n t"))
             nc.vector.quantize_mx(
                 out=w3_codes[:, cols].bitcast(FP8X4),
@@ -159,7 +161,7 @@ def tile_list_qualifier_seed_features_kernel(
 
         def reading(t, c):
             cols = slice(c * CHUNK, (c + 1) * CHUNK)
-            b2 = psum.tile([P, CHUNK], F32, name="b2", tag="short", bufs=2)
+            b2 = psum.tile([P, CHUNK], F32, name="b2", tag="b2", bufs=4)
             for a in range(PASSES):
                 nc.tensor.matmul_mx(
                     out=b2[:],
@@ -170,21 +172,20 @@ def tile_list_qualifier_seed_features_kernel(
                     start=(a == 0),
                     stop=(a == PASSES - 1),
                 )
-            sine = work.tile([P, CHUNK], F32, name="sine", bufs=6)
-            nc.scalar.activation(sine[:], b2[:], ACT.Sin)
-            b1 = psum.tile([P, CHUNK], F32, name="b1", tag="long", bufs=6)
+            nc.scalar.activation(sines[t][:, cols], b2[:], ACT.Sin)
+            b1 = psum.tile([P, CHUNK], F32, name="b1", tag="b1", bufs=4)
             for a in range(PASSES):
                 nc.tensor.matmul_mx(
                     out=b1[:],
-                    lhsT=w1_codes[:, a, t, :].bitcast(FP8X4),
-                    lhsT_scale=w1_plane[:, a, t, :],
+                    lhsT=w1_codes[:, t, a, :].bitcast(FP8X4),
+                    lhsT_scale=w1_plane[:, t, a, :],
                     rhs=v_words[a][c][:].bitcast(FP8X4),
                     rhs_scale=v_scales[:, a, cols],
                     start=(a == 0),
                     stop=(a == PASSES - 1),
                 )
             nc.vector.scalar_tensor_tensor(
-                out=h[t][:, cols], in0=sine[:], scalar=d_cols[:, t : t + 1], in1=b1[:], op0=ALU.mult, op1=ALU.max
+                out=h[t][:, cols], in0=sines[t][:, cols], scalar=d_cols[:, t : t + 1], in1=b1[:], op0=ALU.mult, op1=ALU.max
             )
 
         def pick(key, window, offsets):
@@ -196,11 +197,14 @@ def tile_list_qualifier_seed_features_kernel(
         def pick_and_combine(result, key, window, offsets, op):
             nc.vector.tensor_tensor(result[:], window[:].indirect(offsets), first[key][:], op)
 
-        def smaller(t, j0, j1):
-            nc.vector.tensor_tensor(a3[:, t, j0:j1], first["e", t, j0][:], first["f", t, j0][:], ALU.min)
+        def smaller(t, half):
+            cols = slice(half * HALF, (half + 1) * HALF)
+            nc.vector.tensor_tensor(a3[:, t, cols], first["e", t, half][:], first["f", t, half][:], ALU.min)
 
-        def list_part(tile, j0, j1):
-            return tile[:, j0 // PER_COLUMN : j1 // PER_COLUMN]
+        def pick_last(side, t, half):
+            columns = HALF // PER_COLUMN
+            offsets = {"e": p5, "f": p6}[side][:, half * columns : (half + 1) * columns]
+            pick((side, t, half), a2[t], offsets)
 
         def interleave(half):
             grouped = keep.tile([P, HALF, PACK], BF16, name=f"a3_grouped{half}", align_bytes=64)
@@ -214,7 +218,7 @@ def tile_list_qualifier_seed_features_kernel(
                 out=codes[:].bitcast(FP8X4), scales=plane[:], in_=first["g", half][:].rearrange("p j t -> p (j t)")
             )
             for b in range(OUT_TILES // TILES_PER_BANK):
-                y = psum.tile([P, CHUNK], F32, name="y", tag="short", bufs=2)
+                y = psum.tile([P, CHUNK], F32, name="y", tag=("b1", "b2")[half], bufs=4)
                 for u in range(TILES_PER_BANK):
                     rows = slice((b * TILES_PER_BANK + u) * P, (b * TILES_PER_BANK + u + 1) * P)
                     nc.tensor.matmul_mx(
@@ -226,7 +230,7 @@ def tile_list_qualifier_seed_features_kernel(
                         start=True,
                         stop=True,
                     )
-                result = work.tile([P, TILES_PER_BANK * HALF], F32, name="result", bufs=4)
+                result = work.tile([P, TILES_PER_BANK * HALF], F32, name="result", bufs=6)
                 nc.scalar.activation(result[:], y[:, 0 : TILES_PER_BANK * HALF], ACT.Sigmoid)
                 nc.sync.dma_start(
                     out.rearrange("(u p) j -> p u j", p=P)[
@@ -235,49 +239,57 @@ def tile_list_qualifier_seed_features_kernel(
                     result[:].rearrange("p (u j) -> p u j", j=HALF),
                 )
 
+        prepare(1, 0)
         reading(0, 0)
-        quantise_w1(1, 1, PACK)
-        for c in range(1, CHUNKS):
-            reading(0, c)
+        reading(0, 1)
+        reading(0, 2)
+        reading(0, 3)
         reading(1, 0)
 
         last = PACK - 1
-        for t in range(PACK):
+        pick(("a", 0), h[0], p1[:])
+        reading(1, 1)
+        pick_and_combine(a1[0], ("a", 0), h[0], p2[:], ALU.add)
+        reading(1, 2)
+        reading(1, 3)
+        prepare(2, 0)
+        for t in range(1, PACK):
             pick(("a", t), h[t], p1[:])
-            if t == 0:
-                reading(1, 1)
-            else:
-                pick(("c", t - 1), a1[t - 1], p3[:])
+            pick(("c", t - 1), a1[t - 1], p3[:])
             pick_and_combine(a1[t], ("a", t), h[t], p2[:], ALU.add)
-            if t == 0:
-                reading(1, 2)
-                reading(1, 3)
-                quantise_w3(0)
-                continue
             pick_and_combine(a2[t - 1], ("c", t - 1), a1[t - 1], p4[:], ALU.mult)
             if t < last:
                 reading(t + 1, 0)
-            else:
-                pick(("c", t), a1[t], p3[:])
-            pick(("e", t - 1, 0), a2[t - 1], p5[:])
-            if t == last:
-                pick_and_combine(a2[t], ("c", t), a1[t], p4[:], ALU.mult)
-            pick(("f", t - 1, 0), a2[t - 1], p6[:])
-            if t < last:
+                pick_last("e", t - 1, 0)
+                pick_last("f", t - 1, 0)
                 for c in range(1, CHUNKS):
                     reading(t + 1, c)
-            else:
-                pick(("e", t, 0), a2[t], list_part(p5, 0, HALF))
-            smaller(t - 1, 0, P3)
-            if t == 1:
-                quantise_w3(1)
+                smaller(t - 1, 0)
+                if t + 2 < PACK:
+                    prepare(t + 2, 0)
+                else:
+                    for b in range(W3_PARTS):
+                        quantise_w3(b)
 
-        pick(("f", last, 0), a2[last], list_part(p6, 0, HALF))
-        pick(("e", last, HALF), a2[last], list_part(p5, HALF, P3))
-        smaller(last, 0, HALF)
-        pick(("f", last, HALF), a2[last], list_part(p6, HALF, P3))
+        pick(("c", last), a1[last], p3[:])
+        pick_last("e", last - 1, 0)
+        pick_and_combine(a2[last], ("c", last), a1[last], p4[:], ALU.mult)
+        pick_last("f", last - 1, 0)
+        pick_last("e", last, 0)
+        smaller(last - 1, 0)
+        pick_last("f", last, 0)
+        pick_last("e", 0, 1)
+        smaller(last, 0)
+        pick_last("f", 0, 1)
         interleave(0)
-        smaller(last, HALF, P3)
+        pick_last("e", 1, 1)
+        smaller(0, 1)
         features(0)
+        pick_last("f", 1, 1)
+        for t in range(2, PACK):
+            pick_last("e", t, 1)
+            smaller(t - 1, 1)
+            pick_last("f", t, 1)
+        smaller(last, 1)
         interleave(1)
         features(1)

@@ -18,17 +18,24 @@ ACT = mybir.ActivationFunctionType
 
 P = 128
 PACK = 4
+TILES = H // P
 PASSES = K // (P * PACK)
 CHUNK = 512
 CHUNKS = S // CHUNK
 PER_COLUMN = 16
-SCALE_ROWS = 16
 QUADRANT = 32
+QUADRANTS = P // QUADRANT
+ROWS_PER_QUADRANT = 4
+SCALE_ROWS = QUADRANTS * ROWS_PER_QUADRANT
+FIRST_ROW = P - PASSES * SCALE_ROWS
 HALF = P3 // 2
 OUT_TILES = N // P
 TILES_PER_BANK = 2
-FIRST_ROW = P - PASSES * SCALE_ROWS
 W3_PARTS = 2
+BANKS = 4
+ALIGN = 64
+SYNC_COLUMNS = (2304, 1792)
+MOVES_ON_SYNC = 2
 
 
 def tile_list_qualifier_seed_features_kernel(
@@ -47,180 +54,186 @@ def tile_list_qualifier_seed_features_kernel(
             return tile
 
         idx = load_list("idx", offs)
-        scale_table = keep.tile([P, T // 4], I32, name="scale_table", align_bytes=64)
+
+        scale_table = keep.tile([P, T // 4], I32, name="scale_table", align_bytes=ALIGN)
         nc.sync.dma_start(scale_table[FIRST_ROW:P, :], tab_scales.rearrange("a q t -> (a q) t").bitcast(I32))
-        w2_scales_raw = keep.tile([P, PASSES, H], U8, name="w2_scales_raw", align_bytes=64)
+        w2_scales_raw = keep.tile([P, PASSES, H], U8, name="w2_scales_raw", align_bytes=ALIGN)
         nc.vector.memset(w2_scales_raw[:].bitcast(I32), 0)
         nc.vector.memset(scale_table[0:FIRST_ROW, :], 0)
-        v_scales = keep.tile([P, PASSES, S], U8, name="v_scales", align_bytes=64)
-        nc.vector.memset(v_scales[:].bitcast(I32), 0)
+        v_planes = keep.tile([P, PASSES, S], U8, name="v_planes", align_bytes=ALIGN)
+        nc.vector.memset(v_planes[:].bitcast(I32), 0)
 
         word_tables = [
-            keep.tile([P, T], I32, name=f"word_table{a}", tag=f"table{a}", align_bytes=64) for a in range(PASSES)
+            keep.tile([P, T], I32, name=f"word_table{a}", tag=f"table{a}", align_bytes=ALIGN) for a in range(PASSES)
         ]
         word_rows = [tab_words[a].rearrange("p t i -> p (t i)").bitcast(I32) for a in range(PASSES)]
         for a in range(PASSES):
-            nc.sync.dma_start(word_tables[a][:, 0 : T // 2], word_rows[a][:, 0 : T // 2])
+            nc.sync.dma_start(word_tables[a][:, 0 : SYNC_COLUMNS[a]], word_rows[a][:, 0 : SYNC_COLUMNS[a]])
 
-        w2_raw = keep.tile([P, PASSES, H // 2], I32, name="w2_raw", align_bytes=64)
+        w2_raw = keep.tile([P, PASSES, H // 2], I32, name="w2_raw", align_bytes=ALIGN)
         nc.scalar.dma_start(w2_raw[:], w2_words.rearrange("a p c -> p a c").bitcast(I32))
-        d_cols = keep.tile([P, PACK], F32, name="d_cols")
-        nc.scalar.dma_start(d_cols[:], d.rearrange("(p t) -> p t", t=PACK))
-        for r in range(4):
+        d_cols = keep.tile([P, TILES], F32, name="d_cols")
+        nc.scalar.dma_start(d_cols[:], d.rearrange("(p t) -> p t", t=TILES))
+        for row in range(ROWS_PER_QUADRANT):
             nc.scalar.dma_start(
-                w2_scales_raw[r:P:QUADRANT, :, :].bitcast(I32),
-                w2_scales.rearrange("a (q r) c -> r q a c", r=4)[r].bitcast(I32),
+                w2_scales_raw[row:P:QUADRANT, :, :].bitcast(I32),
+                w2_scales.rearrange("a (quad row) c -> row quad a c", row=ROWS_PER_QUADRANT)[row].bitcast(I32),
             )
         for a in range(PASSES):
-            nc.scalar.dma_start(word_tables[a][:, T // 2 : T], word_rows[a][:, T // 2 : T])
+            nc.scalar.dma_start(word_tables[a][:, SYNC_COLUMNS[a] : T], word_rows[a][:, SYNC_COLUMNS[a] : T])
 
-        picked_scales = keep.tile([P, S], U8, name="picked_scales", align_bytes=64)
+        picked_scales = keep.tile([P, S], U8, name="picked_scales", align_bytes=ALIGN)
         nc.vector.tensor_copy(picked_scales[:], scale_table[:].bitcast(U8).indirect(idx[:]))
         for a in range(PASSES):
-            for q in range(4):
-                row = FIRST_ROW + SCALE_ROWS * a + 4 * q
-                queue = nc.sync if 4 * a + q < 2 else nc.scalar
+            for quad in range(QUADRANTS):
+                source = FIRST_ROW + SCALE_ROWS * a + ROWS_PER_QUADRANT * quad
+                queue = nc.sync if QUADRANTS * a + quad < MOVES_ON_SYNC else nc.scalar
                 queue.dma_start(
-                    v_scales[QUADRANT * q : QUADRANT * q + 4, a, :].bitcast(I32),
-                    picked_scales[row : row + 4, :].bitcast(I32),
+                    v_planes[QUADRANT * quad : QUADRANT * quad + ROWS_PER_QUADRANT, a, :].bitcast(I32),
+                    picked_scales[source : source + ROWS_PER_QUADRANT, :].bitcast(I32),
                 )
 
-        w1_raw = keep.tile([P, PASSES, PACK, H], F32, name="w1_raw", align_bytes=64)
+        w1_raw = keep.tile([P, PASSES, PACK, H], F32, name="w1_raw", align_bytes=ALIGN)
         for a in range(PASSES):
             nc.sync.dma_start(
-                w1_raw[:, a], w1[a * P * PACK : (a + 1) * P * PACK, :].rearrange("(p j) c -> p j c", j=PACK)
+                w1_raw[:, a], w1[a * P * PACK : (a + 1) * P * PACK, :].rearrange("(p i) c -> p i c", i=PACK)
             )
         p1, p2, p3, p4, p5, p6 = [
-            load_list(f"p{i + 1}", source) for i, source in enumerate((pos1, pos2, pos3, pos4, pos5, pos6))
+            load_list(f"p{level + 1}", source) for level, source in enumerate((pos1, pos2, pos3, pos4, pos5, pos6))
         ]
 
         v_words = [[None] * CHUNKS for a in range(PASSES)]
 
-        def pick_words(a, c):
-            picked = keep.tile([P, CHUNK], U32, name=f"v_words{a}_{c}", tag=f"v_words{a}_{c}", align_bytes=64)
+        def pick_words(a, c0, c1):
+            picked = keep.tile([P, (c1 - c0) * CHUNK], U32, name="v_words", tag=f"v_words{a}_{c0}", align_bytes=ALIGN)
             columns = CHUNK // PER_COLUMN
             nc.vector.tensor_copy(
-                picked[:], word_tables[a][:].bitcast(U32).indirect(idx[:, c * columns : (c + 1) * columns])
+                picked[:], word_tables[a][:].bitcast(U32).indirect(idx[:, c0 * columns : c1 * columns])
             )
-            v_words[a][c] = picked
+            for c in range(c0, c1):
+                v_words[a][c] = picked[:, (c - c0) * CHUNK : (c - c0 + 1) * CHUNK]
 
-        w2_plane = keep.tile([P, PASSES, PACK, P], U8, name="w2_plane", align_bytes=64)
-        nc.vector.tensor_copy(w2_plane[:], w2_scales_raw[:].rearrange("p a (m t) -> p a t m", t=PACK))
-        w2_codes = keep.tile([P, PASSES, PACK, P], U16, name="w2_codes", align_bytes=64)
-        nc.vector.tensor_copy(w2_codes[:], w2_raw[:].bitcast(U16).rearrange("p a (m t) -> p a t m", t=PACK))
-        for c in range(CHUNKS):
-            pick_words(0, c)
+        w2_planes = keep.tile([P, PASSES, TILES, P], U8, name="w2_planes", align_bytes=ALIGN)
+        nc.vector.tensor_copy(w2_planes[:], w2_scales_raw[:].rearrange("p a (m t) -> p a t m", t=TILES))
+        w2_codes = keep.tile([P, PASSES, TILES, P], U16, name="w2_codes", align_bytes=ALIGN)
+        nc.vector.tensor_copy(w2_codes[:], w2_raw[:].bitcast(U16).rearrange("p a (m t) -> p a t m", t=TILES))
+        pick_words(0, 0, CHUNKS)
 
-        w1_codes = keep.tile([P, PACK, PASSES, P], U32, name="w1_codes", align_bytes=64)
-        w1_plane = keep.tile([P, PACK, PASSES, P], U8, name="w1_plane", align_bytes=64)
-
+        w1_codes = keep.tile([P, TILES, PASSES, P], U32, name="w1_codes", align_bytes=ALIGN)
+        w1_planes = keep.tile([P, TILES, PASSES, P], U8, name="w1_planes", align_bytes=ALIGN)
         sines = {}
 
         def quantise_w1(t, a0, a1, tag):
-            rounded = keep.tile([P, a1 - a0, P, PACK], BF16, name=f"w1_rounded{t}_{a0}", tag=tag, align_bytes=64)
+            rounded = keep.tile([P, a1 - a0, P, PACK], BF16, name=f"w1_rounded{t}_{a0}", tag=tag, align_bytes=ALIGN)
             for a in range(a0, a1):
-                nc.scalar.copy(rounded[:, a - a0], w1_raw[:, a].rearrange("p j (m t) -> p t m j", t=PACK)[:, t])
+                nc.scalar.copy(rounded[:, a - a0], w1_raw[:, a].rearrange("p i (m t) -> p t m i", t=TILES)[:, t])
             nc.vector.quantize_mx(
                 out=w1_codes[:, t, a0:a1].rearrange("p a m -> p (a m)").bitcast(FP8X4),
-                scales=w1_plane[:, t, a0:a1].rearrange("p a m -> p (a m)"),
-                in_=rounded[:].rearrange("p a m j -> p (a m j)"),
+                scales=w1_planes[:, t, a0:a1].rearrange("p a m -> p (a m)"),
+                in_=rounded[:].rearrange("p a m i -> p (a m i)"),
             )
 
         def prepare(t, a0):
-            quantise_w1(t, a0, PASSES, f"turn{t % 2}")
-            sines[t] = keep.tile([P, S], F32, name=f"sines{t}", tag=f"turn{t % 2}", align_bytes=64)
+            quantise_w1(t, a0, PASSES, f"w1_then_sines{t % 2}")
+            sines[t] = keep.tile([P, S], F32, name=f"sines{t}", tag=f"w1_then_sines{t % 2}", align_bytes=ALIGN)
 
-        pick_words(1, 0)
-        pick_words(1, 1)
-        quantise_w1(0, 0, 1, "v_words1_2")
-        pick_words(1, 2)
-        pick_words(1, 3)
+        middle = CHUNKS // 2
+        pick_words(1, 0, middle)
+        quantise_w1(0, 0, 1, f"v_words1_{middle}")
+        pick_words(1, middle, CHUNKS)
         prepare(0, 1)
 
-        w3_raw = keep.tile([P, PACK, N], F32, name="w3_raw", tag="table0", align_bytes=64)
+        w3_raw = keep.tile([P, PACK, N], F32, name="w3_raw", tag="table0", align_bytes=ALIGN)
         nc.sync.dma_start(w3_raw[:], w3.rearrange("(p t) n -> p t n", t=PACK))
-        w3_codes = keep.tile([P, N], U32, name="w3_codes", align_bytes=64)
-        w3_plane = keep.tile([P, N], U8, name="w3_plane", align_bytes=64)
+        w3_codes = keep.tile([P, N], U32, name="w3_codes", align_bytes=ALIGN)
+        w3_plane = keep.tile([P, N], U8, name="w3_plane", align_bytes=ALIGN)
 
-        def quantise_w3(b):
+        def quantise_w3():
+            rounded = keep.tile([P, N, PACK], BF16, name="w3_rounded", tag="v_words0_0", align_bytes=ALIGN)
             width = N // W3_PARTS
-            cols = slice(b * width, (b + 1) * width)
-            rounded = keep.tile([P, width, PACK], BF16, name=f"w3_rounded{b}", tag=f"v_words0_{b}", align_bytes=64)
-            nc.scalar.copy(rounded[:], w3_raw[:, :, cols].rearrange("p t n -> p n t"))
-            nc.vector.quantize_mx(
-                out=w3_codes[:, cols].bitcast(FP8X4),
-                scales=w3_plane[:, cols],
-                in_=rounded[:].rearrange("p n t -> p (n t)"),
-            )
+            for part in range(W3_PARTS):
+                cols = slice(part * width, (part + 1) * width)
+                nc.scalar.copy(rounded[:, cols, :], w3_raw[:, :, cols].rearrange("p t n -> p n t"))
+                nc.vector.quantize_mx(
+                    out=w3_codes[:, cols].bitcast(FP8X4),
+                    scales=w3_plane[:, cols],
+                    in_=rounded[:, cols, :].rearrange("p n t -> p (n t)"),
+                )
 
-        h = [keep.tile([P, S], F32, name=f"h{t}") for t in range(PACK)]
-        a1 = [keep.tile([P, P1], F32, name=f"a1_{t}") for t in range(PACK)]
-        a2 = [keep.tile([P, P2], F32, name=f"a2_{t}") for t in range(PACK)]
-        a3 = keep.tile([P, PACK, P3], BF16, name="a3", align_bytes=64)
-        first = {}
+        h = [keep.tile([P, S], F32, name=f"h{t}") for t in range(TILES)]
+        a1 = [keep.tile([P, P1], F32, name=f"a1_{t}") for t in range(TILES)]
+        a2 = [keep.tile([P, P2], F32, name=f"a2_{t}") for t in range(TILES)]
+        a3 = keep.tile([P, TILES, P3], BF16, name="a3", align_bytes=ALIGN)
+        gathered = {}
+        a3_words = {}
 
-        def reading(t, c):
+        def first_stage(t, c):
             cols = slice(c * CHUNK, (c + 1) * CHUNK)
-            b2 = psum.tile([P, CHUNK], F32, name="b2", tag="b2", bufs=4)
+            b2 = psum.tile([P, CHUNK], F32, name="b2", tag="b2", bufs=BANKS)
             for a in range(PASSES):
                 nc.tensor.matmul_mx(
                     out=b2[:],
                     lhsT=w2_codes[:, a, t, :].bitcast(U8).bitcast(FP4X4),
-                    lhsT_scale=w2_plane[:, a, t, :],
-                    rhs=v_words[a][c][:].bitcast(FP8X4),
-                    rhs_scale=v_scales[:, a, cols],
+                    lhsT_scale=w2_planes[:, a, t, :],
+                    rhs=v_words[a][c].bitcast(FP8X4),
+                    rhs_scale=v_planes[:, a, cols],
                     start=(a == 0),
                     stop=(a == PASSES - 1),
                 )
             nc.scalar.activation(sines[t][:, cols], b2[:], ACT.Sin)
-            b1 = psum.tile([P, CHUNK], F32, name="b1", tag="b1", bufs=4)
+            b1 = psum.tile([P, CHUNK], F32, name="b1", tag="b1", bufs=BANKS)
             for a in range(PASSES):
                 nc.tensor.matmul_mx(
                     out=b1[:],
                     lhsT=w1_codes[:, t, a, :].bitcast(FP8X4),
-                    lhsT_scale=w1_plane[:, t, a, :],
-                    rhs=v_words[a][c][:].bitcast(FP8X4),
-                    rhs_scale=v_scales[:, a, cols],
+                    lhsT_scale=w1_planes[:, t, a, :],
+                    rhs=v_words[a][c].bitcast(FP8X4),
+                    rhs_scale=v_planes[:, a, cols],
                     start=(a == 0),
                     stop=(a == PASSES - 1),
                 )
             nc.vector.scalar_tensor_tensor(
-                out=h[t][:, cols], in0=sines[t][:, cols], scalar=d_cols[:, t : t + 1], in1=b1[:], op0=ALU.mult, op1=ALU.max
+                out=h[t][:, cols],
+                in0=sines[t][:, cols],
+                scalar=d_cols[:, t : t + 1],
+                in1=b1[:],
+                op0=ALU.mult,
+                op1=ALU.max,
             )
 
         def pick(key, window, offsets):
-            width = offsets.shape[1] * PER_COLUMN
-            picked = work.tile([P, width], F32, name=f"picked_{key[0]}_{width}")
+            picked = work.tile([P, offsets.shape[1] * PER_COLUMN], F32, name=f"picked_{key[0]}")
             nc.vector.tensor_copy(picked[:], window[:].indirect(offsets))
-            first[key] = picked
+            gathered[key] = picked
 
         def pick_and_combine(result, key, window, offsets, op):
-            nc.vector.tensor_tensor(result[:], window[:].indirect(offsets), first[key][:], op)
+            nc.vector.tensor_tensor(result[:], window[:].indirect(offsets), gathered[key][:], op)
+
+        def pick_last(name, t, half):
+            columns = HALF // PER_COLUMN
+            offsets = {"p5": p5, "p6": p6}[name][:, half * columns : (half + 1) * columns]
+            pick((name, t, half), a2[t], offsets)
 
         def smaller(t, half):
             cols = slice(half * HALF, (half + 1) * HALF)
-            nc.vector.tensor_tensor(a3[:, t, cols], first["e", t, half][:], first["f", t, half][:], ALU.min)
+            nc.vector.tensor_tensor(a3[:, t, cols], gathered["p5", t, half][:], gathered["p6", t, half][:], ALU.min)
 
-        def pick_last(side, t, half):
-            columns = HALF // PER_COLUMN
-            offsets = {"e": p5, "f": p6}[side][:, half * columns : (half + 1) * columns]
-            pick((side, t, half), a2[t], offsets)
+        def interleave(half, copy):
+            grouped = keep.tile([P, HALF, PACK], BF16, name=f"a3_grouped{half}", align_bytes=ALIGN)
+            copy(grouped[:], a3[:, :, half * HALF : (half + 1) * HALF].rearrange("p t j -> p j t"))
+            a3_words[half] = grouped
 
-        def interleave(half):
-            grouped = keep.tile([P, HALF, PACK], BF16, name=f"a3_grouped{half}", align_bytes=64)
-            nc.vector.tensor_copy(grouped[:], a3[:, :, half * HALF : (half + 1) * HALF].rearrange("p t j -> p j t"))
-            first["g", half] = grouped
-
-        def features(half):
-            codes = keep.tile([P, HALF], U32, name=f"a3_codes{half}", align_bytes=64)
-            plane = keep.tile([P, HALF], U8, name=f"a3_plane{half}", align_bytes=64)
+        def last_stage(half):
+            codes = keep.tile([P, HALF], U32, name=f"a3_codes{half}", align_bytes=ALIGN)
+            plane = keep.tile([P, HALF], U8, name=f"a3_plane{half}", align_bytes=ALIGN)
             nc.vector.quantize_mx(
-                out=codes[:].bitcast(FP8X4), scales=plane[:], in_=first["g", half][:].rearrange("p j t -> p (j t)")
+                out=codes[:].bitcast(FP8X4), scales=plane[:], in_=a3_words[half][:].rearrange("p j t -> p (j t)")
             )
-            for b in range(OUT_TILES // TILES_PER_BANK):
-                y = psum.tile([P, CHUNK], F32, name="y", tag=("b1", "b2")[half], bufs=4)
+            groups = OUT_TILES // TILES_PER_BANK
+            for group in range(groups):
+                y = psum.tile([P, CHUNK], F32, name="y", tag=("b1", "b2")[half], bufs=BANKS)
                 for u in range(TILES_PER_BANK):
-                    rows = slice((b * TILES_PER_BANK + u) * P, (b * TILES_PER_BANK + u + 1) * P)
+                    rows = slice((group * TILES_PER_BANK + u) * P, (group * TILES_PER_BANK + u + 1) * P)
                     nc.tensor.matmul_mx(
                         out=y[:, u * HALF : (u + 1) * HALF],
                         lhsT=w3_codes[:, rows].bitcast(FP8X4),
@@ -230,66 +243,65 @@ def tile_list_qualifier_seed_features_kernel(
                         start=True,
                         stop=True,
                     )
-                result = work.tile([P, TILES_PER_BANK * HALF], F32, name="result", bufs=6)
+                result = work.tile([P, TILES_PER_BANK * HALF], F32, name="result", bufs=2 * groups)
                 nc.scalar.activation(result[:], y[:, 0 : TILES_PER_BANK * HALF], ACT.Sigmoid)
                 nc.sync.dma_start(
                     out.rearrange("(u p) j -> p u j", p=P)[
-                        :, b * TILES_PER_BANK : (b + 1) * TILES_PER_BANK, half * HALF : (half + 1) * HALF
+                        :, group * TILES_PER_BANK : (group + 1) * TILES_PER_BANK, half * HALF : (half + 1) * HALF
                     ],
                     result[:].rearrange("p (u j) -> p u j", j=HALF),
                 )
 
+        last = TILES - 1
         prepare(1, 0)
-        reading(0, 0)
-        reading(0, 1)
-        reading(0, 2)
-        reading(0, 3)
-        reading(1, 0)
+        for c in range(CHUNKS):
+            first_stage(0, c)
 
-        last = PACK - 1
-        pick(("a", 0), h[0], p1[:])
-        reading(1, 1)
-        pick_and_combine(a1[0], ("a", 0), h[0], p2[:], ALU.add)
-        reading(1, 2)
-        reading(1, 3)
+        first_stage(1, 0)
+        pick(("p1", 0), h[0], p1[:])
+        first_stage(1, 1)
+        pick_and_combine(a1[0], ("p1", 0), h[0], p2[:], ALU.add)
+        for c in range(2, CHUNKS):
+            first_stage(1, c)
         prepare(2, 0)
-        for t in range(1, PACK):
-            pick(("a", t), h[t], p1[:])
-            pick(("c", t - 1), a1[t - 1], p3[:])
-            pick_and_combine(a1[t], ("a", t), h[t], p2[:], ALU.add)
-            pick_and_combine(a2[t - 1], ("c", t - 1), a1[t - 1], p4[:], ALU.mult)
+
+        for t in range(1, TILES):
+            pick(("p1", t), h[t], p1[:])
+            pick(("p3", t - 1), a1[t - 1], p3[:])
+            pick_and_combine(a1[t], ("p1", t), h[t], p2[:], ALU.add)
+            pick_and_combine(a2[t - 1], ("p3", t - 1), a1[t - 1], p4[:], ALU.mult)
             if t < last:
-                reading(t + 1, 0)
-                pick_last("e", t - 1, 0)
-                pick_last("f", t - 1, 0)
+                first_stage(t + 1, 0)
+                pick_last("p5", t - 1, 0)
+                pick_last("p6", t - 1, 0)
                 for c in range(1, CHUNKS):
-                    reading(t + 1, c)
+                    first_stage(t + 1, c)
                 smaller(t - 1, 0)
-                if t + 2 < PACK:
+                if t + 2 < TILES:
                     prepare(t + 2, 0)
                 else:
-                    for b in range(W3_PARTS):
-                        quantise_w3(b)
+                    quantise_w3()
 
-        pick(("c", last), a1[last], p3[:])
-        pick_last("e", last - 1, 0)
-        pick_and_combine(a2[last], ("c", last), a1[last], p4[:], ALU.mult)
-        pick_last("f", last - 1, 0)
-        pick_last("e", last, 0)
+        pick(("p3", last), a1[last], p3[:])
+        pick_last("p5", last - 1, 0)
+        pick_and_combine(a2[last], ("p3", last), a1[last], p4[:], ALU.mult)
+        pick_last("p6", last - 1, 0)
+        pick_last("p5", last, 0)
         smaller(last - 1, 0)
-        pick_last("f", last, 0)
-        pick_last("e", 0, 1)
+        pick_last("p6", last, 0)
+
+        pick_last("p5", 0, 1)
         smaller(last, 0)
-        pick_last("f", 0, 1)
-        interleave(0)
-        pick_last("e", 1, 1)
+        pick_last("p6", 0, 1)
+        interleave(0, nc.scalar.copy)
+        pick_last("p5", 1, 1)
         smaller(0, 1)
-        features(0)
-        pick_last("f", 1, 1)
-        for t in range(2, PACK):
-            pick_last("e", t, 1)
+        last_stage(0)
+        pick_last("p6", 1, 1)
+        for t in range(2, TILES):
+            pick_last("p5", t, 1)
             smaller(t - 1, 1)
-            pick_last("f", t, 1)
+            pick_last("p6", t, 1)
         smaller(last, 1)
-        interleave(1)
-        features(1)
+        interleave(1, nc.vector.tensor_copy)
+        last_stage(1)

from contextlib import ExitStack

import concourse.mybir as mybir

K, H, N, T, S, P1, P2, P3 = 1024, 512, 768, 4096, 2048, 1024, 512, 256
FLOPS = 2 * (2 * K * H * S + H * N * P3)

F32 = mybir.dt.float32
BF16 = mybir.dt.bfloat16
I32 = mybir.dt.int32
U32 = mybir.dt.uint32
U16 = mybir.dt.uint16
U8 = mybir.dt.uint8
FP8X4 = mybir.dt.float8_e4m3fn_x4
FP4X4 = mybir.dt.float4_e2m1fn_x4
ALU = mybir.AluOpType
ACT = mybir.ActivationFunctionType

P = 128
PACK = 4
TILES = H // P
PASSES = K // (P * PACK)
CHUNK = 512
CHUNKS = S // CHUNK
PER_COLUMN = 16
QUADRANT = 32
QUADRANTS = P // QUADRANT
ROWS_PER_QUADRANT = 4
SCALE_ROWS = QUADRANTS * ROWS_PER_QUADRANT
FIRST_ROW = P - PASSES * SCALE_ROWS
HALF = P3 // 2
OUT_TILES = N // P
TILES_PER_BANK = 2
W3_PARTS = 2
BANKS = 4
ALIGN = 64
SYNC_COLUMNS = (2304, 1792)
MOVES_ON_SYNC = 2


def tile_list_qualifier_seed_features_kernel(
    tc, tab_words, tab_scales, offs, w1, w2_words, w2_scales, d, pos1, pos2, pos3, pos4, pos5, pos6, w3, out
):
    nc = tc.nc
    with ExitStack() as ctx:
        lists = ctx.enter_context(tc.tile_pool(name="lists", bufs=1))
        keep = ctx.enter_context(tc.tile_pool(name="keep", bufs=1))
        work = ctx.enter_context(tc.tile_pool(name="work", bufs=2))
        psum = ctx.enter_context(tc.psum_pool(name="psum", bufs=1))

        def load_list(name, source):
            tile = lists.tile(list(source.shape), U16, name=name)
            nc.sync.dma_start(tile[:], source)
            return tile

        idx = load_list("idx", offs)

        scale_table = keep.tile([P, T // 4], I32, name="scale_table", align_bytes=ALIGN)
        nc.sync.dma_start(scale_table[FIRST_ROW:P, :], tab_scales.rearrange("a q t -> (a q) t").bitcast(I32))
        w2_scales_raw = keep.tile([P, PASSES, H], U8, name="w2_scales_raw", align_bytes=ALIGN)
        nc.vector.memset(w2_scales_raw[:].bitcast(I32), 0)
        nc.vector.memset(scale_table[0:FIRST_ROW, :], 0)
        v_planes = keep.tile([P, PASSES, S], U8, name="v_planes", align_bytes=ALIGN)
        nc.vector.memset(v_planes[:].bitcast(I32), 0)

        word_tables = [
            keep.tile([P, T], I32, name=f"word_table{a}", tag=f"table{a}", align_bytes=ALIGN) for a in range(PASSES)
        ]
        word_rows = [tab_words[a].rearrange("p t i -> p (t i)").bitcast(I32) for a in range(PASSES)]
        for a in range(PASSES):
            nc.sync.dma_start(word_tables[a][:, 0 : SYNC_COLUMNS[a]], word_rows[a][:, 0 : SYNC_COLUMNS[a]])

        w2_raw = keep.tile([P, PASSES, H // 2], I32, name="w2_raw", align_bytes=ALIGN)
        nc.scalar.dma_start(w2_raw[:], w2_words.rearrange("a p c -> p a c").bitcast(I32))
        d_cols = keep.tile([P, TILES], F32, name="d_cols")
        nc.scalar.dma_start(d_cols[:], d.rearrange("(p t) -> p t", t=TILES))
        for row in range(ROWS_PER_QUADRANT):
            nc.scalar.dma_start(
                w2_scales_raw[row:P:QUADRANT, :, :].bitcast(I32),
                w2_scales.rearrange("a (quad row) c -> row quad a c", row=ROWS_PER_QUADRANT)[row].bitcast(I32),
            )
        for a in range(PASSES):
            nc.scalar.dma_start(word_tables[a][:, SYNC_COLUMNS[a] : T], word_rows[a][:, SYNC_COLUMNS[a] : T])

        picked_scales = keep.tile([P, S], U8, name="picked_scales", align_bytes=ALIGN)
        nc.vector.tensor_copy(picked_scales[:], scale_table[:].bitcast(U8).indirect(idx[:]))
        for a in range(PASSES):
            for quad in range(QUADRANTS):
                source = FIRST_ROW + SCALE_ROWS * a + ROWS_PER_QUADRANT * quad
                queue = nc.sync if QUADRANTS * a + quad < MOVES_ON_SYNC else nc.scalar
                queue.dma_start(
                    v_planes[QUADRANT * quad : QUADRANT * quad + ROWS_PER_QUADRANT, a, :].bitcast(I32),
                    picked_scales[source : source + ROWS_PER_QUADRANT, :].bitcast(I32),
                )

        w1_raw = keep.tile([P, PASSES, PACK, H], F32, name="w1_raw", align_bytes=ALIGN)
        for a in range(PASSES):
            nc.sync.dma_start(
                w1_raw[:, a], w1[a * P * PACK : (a + 1) * P * PACK, :].rearrange("(p i) c -> p i c", i=PACK)
            )
        p1, p2, p3, p4, p5, p6 = [
            load_list(f"p{level + 1}", source) for level, source in enumerate((pos1, pos2, pos3, pos4, pos5, pos6))
        ]

        v_words = [[None] * CHUNKS for a in range(PASSES)]

        def pick_words(a, c0, c1):
            picked = keep.tile([P, (c1 - c0) * CHUNK], U32, name="v_words", tag=f"v_words{a}_{c0}", align_bytes=ALIGN)
            columns = CHUNK // PER_COLUMN
            nc.vector.tensor_copy(
                picked[:], word_tables[a][:].bitcast(U32).indirect(idx[:, c0 * columns : c1 * columns])
            )
            for c in range(c0, c1):
                v_words[a][c] = picked[:, (c - c0) * CHUNK : (c - c0 + 1) * CHUNK]

        w2_planes = keep.tile([P, PASSES, TILES, P], U8, name="w2_planes", align_bytes=ALIGN)
        nc.vector.tensor_copy(w2_planes[:], w2_scales_raw[:].rearrange("p a (m t) -> p a t m", t=TILES))
        w2_codes = keep.tile([P, PASSES, TILES, P], U16, name="w2_codes", align_bytes=ALIGN)
        nc.vector.tensor_copy(w2_codes[:], w2_raw[:].bitcast(U16).rearrange("p a (m t) -> p a t m", t=TILES))
        pick_words(0, 0, CHUNKS)

        w1_codes = keep.tile([P, TILES, PASSES, P], U32, name="w1_codes", align_bytes=ALIGN)
        w1_planes = keep.tile([P, TILES, PASSES, P], U8, name="w1_planes", align_bytes=ALIGN)
        sines = {}

        def quantise_w1(t, a0, a1, tag):
            rounded = keep.tile([P, a1 - a0, P, PACK], BF16, name=f"w1_rounded{t}_{a0}", tag=tag, align_bytes=ALIGN)
            for a in range(a0, a1):
                nc.scalar.copy(rounded[:, a - a0], w1_raw[:, a].rearrange("p i (m t) -> p t m i", t=TILES)[:, t])
            nc.vector.quantize_mx(
                out=w1_codes[:, t, a0:a1].rearrange("p a m -> p (a m)").bitcast(FP8X4),
                scales=w1_planes[:, t, a0:a1].rearrange("p a m -> p (a m)"),
                in_=rounded[:].rearrange("p a m i -> p (a m i)"),
            )

        def prepare(t, a0):
            quantise_w1(t, a0, PASSES, f"w1_then_sines{t % 2}")
            sines[t] = keep.tile([P, S], F32, name=f"sines{t}", tag=f"w1_then_sines{t % 2}", align_bytes=ALIGN)

        middle = CHUNKS // 2
        pick_words(1, 0, middle)
        quantise_w1(0, 0, 1, f"v_words1_{middle}")
        pick_words(1, middle, CHUNKS)
        prepare(0, 1)

        w3_raw = keep.tile([P, PACK, N], F32, name="w3_raw", tag="table0", align_bytes=ALIGN)
        nc.sync.dma_start(w3_raw[:], w3.rearrange("(p t) n -> p t n", t=PACK))
        w3_codes = keep.tile([P, N], U32, name="w3_codes", align_bytes=ALIGN)
        w3_plane = keep.tile([P, N], U8, name="w3_plane", align_bytes=ALIGN)

        def quantise_w3():
            rounded = keep.tile([P, N, PACK], BF16, name="w3_rounded", tag="v_words0_0", align_bytes=ALIGN)
            width = N // W3_PARTS
            for part in range(W3_PARTS):
                cols = slice(part * width, (part + 1) * width)
                nc.scalar.copy(rounded[:, cols, :], w3_raw[:, :, cols].rearrange("p t n -> p n t"))
                nc.vector.quantize_mx(
                    out=w3_codes[:, cols].bitcast(FP8X4),
                    scales=w3_plane[:, cols],
                    in_=rounded[:, cols, :].rearrange("p n t -> p (n t)"),
                )

        h = [keep.tile([P, S], F32, name=f"h{t}") for t in range(TILES)]
        a1 = [keep.tile([P, P1], F32, name=f"a1_{t}") for t in range(TILES)]
        a2 = [keep.tile([P, P2], F32, name=f"a2_{t}") for t in range(TILES)]
        a3 = keep.tile([P, TILES, P3], BF16, name="a3", align_bytes=ALIGN)
        gathered = {}
        a3_words = {}

        def first_stage(t, c):
            cols = slice(c * CHUNK, (c + 1) * CHUNK)
            b2 = psum.tile([P, CHUNK], F32, name="b2", tag="b2", bufs=BANKS)
            for a in range(PASSES):
                nc.tensor.matmul_mx(
                    out=b2[:],
                    lhsT=w2_codes[:, a, t, :].bitcast(U8).bitcast(FP4X4),
                    lhsT_scale=w2_planes[:, a, t, :],
                    rhs=v_words[a][c].bitcast(FP8X4),
                    rhs_scale=v_planes[:, a, cols],
                    start=(a == 0),
                    stop=(a == PASSES - 1),
                )
            nc.scalar.activation(sines[t][:, cols], b2[:], ACT.Sin)
            b1 = psum.tile([P, CHUNK], F32, name="b1", tag="b1", bufs=BANKS)
            for a in range(PASSES):
                nc.tensor.matmul_mx(
                    out=b1[:],
                    lhsT=w1_codes[:, t, a, :].bitcast(FP8X4),
                    lhsT_scale=w1_planes[:, t, a, :],
                    rhs=v_words[a][c].bitcast(FP8X4),
                    rhs_scale=v_planes[:, a, cols],
                    start=(a == 0),
                    stop=(a == PASSES - 1),
                )
            nc.vector.scalar_tensor_tensor(
                out=h[t][:, cols],
                in0=sines[t][:, cols],
                scalar=d_cols[:, t : t + 1],
                in1=b1[:],
                op0=ALU.mult,
                op1=ALU.max,
            )

        def pick(key, window, offsets):
            picked = work.tile([P, offsets.shape[1] * PER_COLUMN], F32, name=f"picked_{key[0]}")
            nc.vector.tensor_copy(picked[:], window[:].indirect(offsets))
            gathered[key] = picked

        def pick_and_combine(result, key, window, offsets, op):
            nc.vector.tensor_tensor(result[:], window[:].indirect(offsets), gathered[key][:], op)

        def pick_last(name, t, half):
            columns = HALF // PER_COLUMN
            offsets = {"p5": p5, "p6": p6}[name][:, half * columns : (half + 1) * columns]
            pick((name, t, half), a2[t], offsets)

        def smaller(t, half):
            cols = slice(half * HALF, (half + 1) * HALF)
            nc.vector.tensor_tensor(a3[:, t, cols], gathered["p5", t, half][:], gathered["p6", t, half][:], ALU.min)

        def interleave(half, copy):
            grouped = keep.tile([P, HALF, PACK], BF16, name=f"a3_grouped{half}", align_bytes=ALIGN)
            copy(grouped[:], a3[:, :, half * HALF : (half + 1) * HALF].rearrange("p t j -> p j t"))
            a3_words[half] = grouped

        def last_stage(half):
            codes = keep.tile([P, HALF], U32, name=f"a3_codes{half}", align_bytes=ALIGN)
            plane = keep.tile([P, HALF], U8, name=f"a3_plane{half}", align_bytes=ALIGN)
            nc.vector.quantize_mx(
                out=codes[:].bitcast(FP8X4), scales=plane[:], in_=a3_words[half][:].rearrange("p j t -> p (j t)")
            )
            groups = OUT_TILES // TILES_PER_BANK
            for group in range(groups):
                y = psum.tile([P, CHUNK], F32, name="y", tag=("b1", "b2")[half], bufs=BANKS)
                for u in range(TILES_PER_BANK):
                    rows = slice((group * TILES_PER_BANK + u) * P, (group * TILES_PER_BANK + u + 1) * P)
                    nc.tensor.matmul_mx(
                        out=y[:, u * HALF : (u + 1) * HALF],
                        lhsT=w3_codes[:, rows].bitcast(FP8X4),
                        lhsT_scale=w3_plane[:, rows],
                        rhs=codes[:].bitcast(FP8X4),
                        rhs_scale=plane[:],
                        start=True,
                        stop=True,
                    )
                result = work.tile([P, TILES_PER_BANK * HALF], F32, name="result", bufs=2 * groups)
                nc.scalar.activation(result[:], y[:, 0 : TILES_PER_BANK * HALF], ACT.Sigmoid)
                nc.sync.dma_start(
                    out.rearrange("(u p) j -> p u j", p=P)[
                        :, group * TILES_PER_BANK : (group + 1) * TILES_PER_BANK, half * HALF : (half + 1) * HALF
                    ],
                    result[:].rearrange("p (u j) -> p u j", j=HALF),
                )

        last = TILES - 1
        prepare(1, 0)
        for c in range(CHUNKS):
            first_stage(0, c)

        first_stage(1, 0)
        pick(("p1", 0), h[0], p1[:])
        first_stage(1, 1)
        pick_and_combine(a1[0], ("p1", 0), h[0], p2[:], ALU.add)
        for c in range(2, CHUNKS):
            first_stage(1, c)
        prepare(2, 0)

        for t in range(1, TILES):
            pick(("p1", t), h[t], p1[:])
            pick(("p3", t - 1), a1[t - 1], p3[:])
            pick_and_combine(a1[t], ("p1", t), h[t], p2[:], ALU.add)
            pick_and_combine(a2[t - 1], ("p3", t - 1), a1[t - 1], p4[:], ALU.mult)
            if t < last:
                first_stage(t + 1, 0)
                pick_last("p5", t - 1, 0)
                pick_last("p6", t - 1, 0)
                for c in range(1, CHUNKS):
                    first_stage(t + 1, c)
                smaller(t - 1, 0)
                if t + 2 < TILES:
                    prepare(t + 2, 0)
                else:
                    quantise_w3()

        pick(("p3", last), a1[last], p3[:])
        pick_last("p5", last - 1, 0)
        pick_and_combine(a2[last], ("p3", last), a1[last], p4[:], ALU.mult)
        pick_last("p6", last - 1, 0)
        pick_last("p5", last, 0)
        smaller(last - 1, 0)
        pick_last("p6", last, 0)

        pick_last("p5", 0, 1)
        smaller(last, 0)
        pick_last("p6", 0, 1)
        interleave(0, nc.scalar.copy)
        pick_last("p5", 1, 1)
        smaller(0, 1)
        last_stage(0)
        pick_last("p6", 1, 1)
        for t in range(2, TILES):
            pick_last("p5", t, 1)
            smaller(t - 1, 1)
            pick_last("p6", t, 1)
        smaller(last, 1)
        interleave(1, nc.vector.tensor_copy)
        last_stage(1)
